import numpy as np
import ml_dtypes


def mxq(x, axis, fmt="e4m3"):
    dtype, down = {"e4m3": (ml_dtypes.float8_e4m3fn, 7), "e5m2": (ml_dtypes.float8_e5m2, 14)}[fmt]
    v = np.moveaxis(np.asarray(x, np.float32).astype(ml_dtypes.bfloat16).astype(np.float64), axis, -1)
    blocks = v.reshape(v.shape[:-1] + (-1, 32))
    amax = np.abs(blocks).max(-1, keepdims=True)
    byte = np.maximum(np.where(amax > 0, np.frexp(amax)[1] - 1 + 127, 0) - down, 1)
    scale = np.exp2(byte - 127.0)
    codes = (blocks / scale).astype(np.float32).astype(dtype).astype(np.float64)
    return np.moveaxis((codes * scale).reshape(v.shape), -1, axis)


WIDE = False


def mx_kscale(k):
    if not WIDE:
        return np.ones(k)
    levels = np.array([10, -10, 5, -5, 0])
    if k % 512:
        return np.exp2(np.random.permutation(np.resize(levels, k // 32))).repeat(32)
    a = np.empty((k // 512, 16))
    for p in range(k // 512):
        a[p, :8] = np.random.permutation(np.resize(levels, 8))
        for g in range(8):
            far = levels[np.abs(levels - a[p, g]) >= 10]
            a[p, g + 8] = far[np.random.randint(len(far))]
    return np.exp2(a.ravel()).repeat(32)


def f64(x):
    return np.asarray(x).astype(np.float64)


def striped(idx):
    return np.tile(idx.reshape(-1, 16).T, (8, 1)).astype(np.uint16)


def unstriped(offs):
    return offs[:16].T.reshape(-1).astype(np.int64)


E2M1 = np.array([0.0, 0.5, 1.0, 1.5, 2.0, 3.0, 4.0, 6.0, -0.0, -0.5, -1.0, -1.5, -2.0, -3.0, -4.0, -6.0])


def pack_weight(w, fmt):
    k, n = w.shape
    w = f64(np.asarray(w, np.float32).astype(ml_dtypes.bfloat16)).reshape(k // 32, 32, n)
    amax = np.abs(w).max(1)
    if fmt == "e4m3":
        byte = np.frexp(amax)[1] - 1 + 127 - 7
    else:
        mant, ex = np.frexp(amax / 6.0)
        byte = np.where(mant > 0.5, ex, ex - 1) + 127
    byte = np.clip(np.where(amax > 0, byte, 1), 1, 254)
    scaled = (w * np.exp2(127.0 - byte)[:, None, :]).reshape(k, n).astype(np.float32)
    by_word = np.ascontiguousarray(scaled.reshape(k // 512, 128, 4, n).transpose(0, 1, 3, 2))
    if fmt == "e4m3":
        words = by_word.astype(ml_dtypes.float8_e4m3fn).view(np.uint8)
    else:
        c = by_word.astype(ml_dtypes.float4_e2m1fn).view(np.uint8) & 0xF
        words = (c[..., 0::2] | (c[..., 1::2] << 4)).reshape(k // 512, 128, 2 * n)
    return np.ascontiguousarray(words), np.ascontiguousarray(byte.astype(np.uint8).reshape(k // 512, 16, n))


def unpack_weight(words, scales, fmt):
    g, _, n = scales.shape
    words = np.ascontiguousarray(words).reshape(g, 128, n, -1)
    if fmt == "e4m3":
        vals = words.view(ml_dtypes.float8_e4m3fn).astype(np.float64)
    else:
        nib = np.empty((g, 128, n, 4), np.uint8)
        nib[..., 0::2] = words & 0xF
        nib[..., 1::2] = words >> 4
        vals = E2M1[nib]
    vals = vals * np.repeat(np.exp2(scales.astype(np.float64) - 127.0), 8, axis=1)[..., None]
    return vals.transpose(0, 1, 3, 2).reshape(g * 512, n)


def gelu(v):
    return 0.5 * v * (1.0 + np.tanh(np.sqrt(2.0 / np.pi) * (v + 0.044715 * v**3)))


def bf(x):
    return np.asarray(x, np.float32).astype(ml_dtypes.bfloat16)


def planes(Y):
    n, m = Y.shape
    b = f64(bf(Y)).reshape(n // 32, 32, m)
    amax = np.abs(b).max(1)
    byte = np.clip(np.where(amax > 0, np.frexp(amax)[1] - 1 + 127 - 7, 1), 1, 254)
    codes = (b * np.exp2(127.0 - byte)[:, None, :]).reshape(n, m).astype(np.float32).astype(ml_dtypes.float8_e4m3fn).view(np.uint8)
    words = codes.reshape(n // 512, 128, 4, m).transpose(0, 1, 3, 2)
    return np.ascontiguousarray(words), np.ascontiguousarray(byte.astype(np.uint8).reshape(n // 512, 16, m))


K, H, N, T, S, T2, P = 1536, 1024, 384, 2048, 512, 1024, 512

def setup_inputs():
    n = np.random.standard_normal
    s = mx_kscale(K)[:, None]
    u = mx_kscale(H)[:, None]
    d = {}
    d["tab_words"], d["tab_scales"] = pack_weight(n((K, T)) * s, "e4m3")
    d["offs"] = striped(np.random.permutation(T)[:S])
    d["offs2"] = striped(np.random.permutation(T2)[:S])
    d["offs3"] = striped(np.random.permutation(T2)[:P])
    d["w1"] = (n((K, H)) / K**0.5 / s * u.T).astype(np.float32)
    d["b1"] = (0.5 * n(H) * u[:, 0]).astype(np.float32)
    d["w2_words"], d["w2_scales"] = pack_weight(n((K, H)) / K**0.5 / s * u.T, "e2m1")
    d["wgs"] = np.exp(0.3 * n((128, S))).astype(np.float32)
    d["page0"] = (n((H, T2)) * u).astype(np.float32)
    d["lens"] = np.exp(0.4 * n(H)).astype(np.float32)
    d["w3"] = (1.5 * n((H, N)) / H**0.5 / u).astype(np.float32)
    d["b3"] = (0.6 * n(N)).astype(np.float32)
    return d

def reference(tab_words, tab_scales, offs, offs2, offs3, w1, b1, w2_words, w2_scales, wgs, page0, lens, w3, b3):
    v = unpack_weight(tab_words, tab_scales, "e4m3")[:, unstriped(offs)]
    w2 = unpack_weight(w2_words, w2_scales, "e2m1")
    symptom = (mxq(f64(w1), 0, "e4m3").T @ v) + f64(b1)[:, None]
    context = w2.T @ v
    h = np.maximum(symptom, context)
    page = f64(page0).copy()
    page[:, unstriped(offs2)] = np.tile(f64(wgs), (H // 128, 1)) * h
    x = f64(lens)[:, None] * page[:, unstriped(offs3)]
    e = mxq(f64(w3), 0, "e4m3").T @ mxq(x, 0, "e4m3")
    y = 1.0 / (1.0 + np.exp(-(e + f64(b3)[:, None])))
    words, scales = planes(page)
    return y, page, words, scales

@@ -1,0 +1,389 @@
+from contextlib import ExitStack
+
+import concourse.mybir as mybir
+
+K, H, N, T, S, T2, PICK = 1536, 1024, 384, 2048, 512, 1024, 512
+FLOPS = 2 * (2 * K * H * S + H * N * PICK)
+
+F32 = mybir.dt.float32
+BF16 = mybir.dt.bfloat16
+I32 = mybir.dt.int32
+U32 = mybir.dt.uint32
+U16 = mybir.dt.uint16
+U8 = mybir.dt.uint8
+FP8X4 = mybir.dt.float8_e4m3fn_x4
+FP4X4 = mybir.dt.float4_e2m1fn_x4
+ALU = mybir.AluOpType
+ACT = mybir.ActivationFunctionType
+
+P = 128
+PACK = 4
+K_PASS = P * PACK
+PASSES = K // K_PASS
+GROUPS = H // K_PASS
+TILES = GROUPS * PACK
+N_TILES = N // P
+QUADS = 4
+QUAD = 32
+
+
+def tile_list_triage_urgency_marks_kernel(
+    tc, tab_words, tab_scales, offs, offs2, offs3, w1, b1, w2_words, w2_scales, wgs, page0, lens, w3, b3,
+    out_0, out_1, out_2, out_3,
+):
+    nc = tc.nc
+    with ExitStack() as ctx:
+        lists = ctx.enter_context(tc.tile_pool(name="lists", bufs=1))
+        keep = ctx.enter_context(tc.tile_pool(name="keep", bufs=1))
+        psum = ctx.enter_context(tc.psum_pool(name="psum", bufs=1))
+
+        def sb(name, shape, dtype, tag=None, bufs=1, pool=keep):
+            return pool.tile(shape, dtype, name=name, tag=tag or name, bufs=bufs, align_bytes=64)
+
+        idx = lists.tile([P, S // 16], U16, name="idx")
+        idx2 = lists.tile([P, S // 16], U16, name="idx2")
+        idx3 = lists.tile([P, PICK // 16], U16, name="idx3")
+
+        tab_sc = sb("tab_sc", [P, PASSES, T], U8)
+        w2_sc_raw = sb("w2_sc_raw", [P, PASSES, H], U8)
+        nc.vector.memset(tab_sc[:].bitcast(I32), 0)
+        nc.vector.memset(w2_sc_raw[:].bitcast(I32), 0)
+
+        warm = sb("warm", [P, 8], F32)
+        nc.vector.memset(warm[:], 0.0)
+        nc.scalar.activation(out=warm[:, 1:2], in_=warm[:, 0:1], func=ACT.Sigmoid)
+
+        w1_raw = {}
+
+        def load_w1(g, a, pool):
+            raw = sb("w1_raw_%d_%d" % (g, a), [P, PACK, K_PASS], F32, tag="stage_%d_%d" % (g, a), pool=pool)
+            rows = w1[a * K_PASS : (a + 1) * K_PASS, g * K_PASS : (g + 1) * K_PASS]
+            nc.sync.dma_start(out=raw[:], in_=rows.rearrange("(p j) c -> p j c", j=PACK))
+            w1_raw[g, a] = raw
+
+        tab = {}
+
+        def load_tab(a):
+            words = sb("tab_%d" % a, [P, T], I32, pool=late)
+            nc.sync.dma_start(out=words[:], in_=tab_words[a].rearrange("p t i -> p (t i)").bitcast(I32))
+            tab[a] = words
+
+        page = {}
+        page_rows = page0.rearrange("(g p t) m -> g t p m", p=P, t=PACK)
+        out_rows = out_1.rearrange("(g p t) m -> g t p m", p=P, t=PACK)
+
+        def load_page(k):
+            page[k] = sb("page_%d" % k, [P, T2], F32, pool=late)
+            nc.sync.dma_start(out=page[k][:], in_=page_rows[k // PACK, k % PACK])
+
+        wgs_rows = wgs.rearrange("(q t) j -> q t j", t=PACK)
+        wgs_sb = {}
+
+        def load_wgs(t0, t1):
+            part = sb("wgs_%d" % t0, [P, t1 - t0, S], F32, pool=late)
+            for q in (0, 2, 1, 3):
+                nc.sync.dma_start(out=part[QUAD * q : QUAD * (q + 1), :, :], in_=wgs_rows[:, t0:t1, :])
+            for t in range(t0, t1):
+                wgs_sb[t] = part[:, t - t0, :]
+
+        w2_codes, w2_sc = {}, {}
+
+        def deal_w2_words(g):
+            w2_codes[g] = sb("w2_codes_%d" % g, [P, PASSES, K_PASS * 2], U8)
+            nc.vector.tensor_copy(
+                out=w2_codes[g][:].bitcast(U16).rearrange("p a (t h i) -> p h a t i", t=PACK, i=8),
+                in_=w2_raw[g][:].bitcast(U16).rearrange("p a (h i t) -> p h a t i", t=PACK, i=8),
+            )
+
+        with tc.tile_pool(name="early", bufs=1) as early:
+            w2_raw = {}
+            for g in range(GROUPS):
+                w2_raw[g] = sb("w2_raw_%d" % g, [P, PASSES, K_PASS // 2], I32, pool=early if g == 0 else keep)
+                words = w2_words[:, :, g * 2 * K_PASS : (g + 1) * 2 * K_PASS]
+                nc.sync.dma_start(out=w2_raw[g][:], in_=words.bitcast(I32).rearrange("a p c -> p a c"))
+            nc.sync.dma_start(idx[:], offs)
+            nc.sync.dma_start(idx2[:], offs2)
+            nc.sync.dma_start(idx3[:], offs3)
+            for q in range(QUADS):
+                nc.sync.dma_start(
+                    out=tab_sc[QUAD * q : QUAD * q + 4, :, :].bitcast(I32),
+                    in_=tab_scales[:, 4 * q : 4 * q + 4, :].bitcast(I32).rearrange("a r t -> r a t"),
+                )
+            for q in range(QUADS):
+                nc.sync.dma_start(
+                    out=w2_sc_raw[QUAD * q : QUAD * q + 4, :, :].bitcast(I32),
+                    in_=w2_scales[:, 4 * q : 4 * q + 4, :].bitcast(I32).rearrange("a r c -> r a c"),
+                )
+            deal_w2_words(0)
+        deal_w2_words(1)
+        late = ctx.enter_context(tc.tile_pool(name="late", bufs=1))
+        load_w1(0, 0, late)
+        load_w1(0, 1, late)
+        load_tab(0)
+        load_w1(0, 2, late)
+        load_tab(1)
+        load_tab(2)
+        b1_sb = sb("b1_sb", [P, GROUPS, PACK], F32, pool=late)
+        nc.sync.dma_start(out=b1_sb[:], in_=b1.rearrange("(g p t) -> p g t", p=P, t=PACK))
+        load_page(0)
+        load_wgs(0, 1)
+        load_page(1)
+        lens_sb = sb("lens_sb", [P, GROUPS, PACK], F32, pool=late)
+        nc.sync.dma_start(out=lens_sb[:], in_=lens.rearrange("(g p t) -> p g t", p=P, t=PACK))
+        b3_sb = sb("b3_sb", [P, N_TILES], F32, pool=late)
+        nc.sync.dma_start(out=b3_sb[:], in_=b3.rearrange("(p c) -> p c", c=N_TILES))
+        load_wgs(1, 2)
+        load_w1(1, 0, late)
+        load_wgs(2, 4)
+        load_page(2)
+        load_w1(1, 1, late)
+        load_w1(1, 2, late)
+        load_page(3)
+        load_page(4)
+        w3_raw = {}
+        for g in range(GROUPS):
+            rows = w3[g * K_PASS : (g + 1) * K_PASS, :]
+            w3_raw[g] = sb("w3_raw_%d" % g, [P, PACK, N], F32, pool=late)
+            nc.sync.dma_start(out=w3_raw[g][:], in_=rows.rearrange("(p j) n -> p j n", j=PACK))
+        for k in range(5, TILES):
+            load_page(k)
+
+        w1_codes, w1_sc, w1_bf = {}, {}, {}
+
+        def round_w1(g, a):
+            w1_bf[g, a] = sb("w1_bf_%d_%d" % (g, a), [P, K_PASS * PACK], BF16, tag="w1_bf", bufs=2)
+            nc.scalar.copy(
+                out=w1_bf[g, a][:].rearrange("p (t m j) -> p m t j", t=PACK, j=PACK),
+                in_=w1_raw[g, a][:].rearrange("p j (m t) -> p m t j", t=PACK),
+            )
+
+        def quantize_w1(g, a):
+            w1_codes[g, a] = sb("w1_codes_%d_%d" % (g, a), [P, K_PASS], U32)
+            w1_sc[g, a] = sb("w1_sc_%d_%d" % (g, a), [P, K_PASS], U8)
+            nc.vector.quantize_mx(out=w1_codes[g, a][:].bitcast(FP8X4), scales=w1_sc[g, a][:], in_=w1_bf[g, a][:])
+
+        v_codes, v_sc = {}, {}
+
+        def gather_scales(a):
+            v_sc[a] = sb("v_sc_%d" % a, [P, S], U8)
+            nc.vector.tensor_copy(v_sc[a][:], tab_sc[:, a, :].indirect(idx[:]))
+
+        def gather_words(a):
+            v_codes[a] = sb("v_codes_%d" % a, [P, S], U32)
+            nc.vector.tensor_copy(v_codes[a][:], tab[a][:].bitcast(U32).indirect(idx[:]))
+
+        def deal_w2_scales(g):
+            w2_sc[g] = sb("w2_sc_%d" % g, [P, PASSES, K_PASS], U8, tag="tab_2" if g else None, pool=late)
+            nc.vector.tensor_copy(
+                out=w2_sc[g][:].rearrange("p a (t h i) -> p h a t i", t=PACK, i=16),
+                in_=w2_sc_raw[:, :, g * K_PASS : (g + 1) * K_PASS].rearrange("p a (h i t) -> p h a t i", t=PACK, i=16),
+            )
+
+        for a in range(PASSES):
+            gather_scales(a)
+        deal_w2_scales(0)
+        for a in range(PASSES):
+            round_w1(0, a)
+            quantize_w1(0, a)
+            gather_words(a)
+        deal_w2_scales(1)
+
+        h, picked, sym_ps, ctx_sb = {}, {}, {}, {}
+
+        def first_stage(k):
+            g, t = divmod(k, PACK)
+            ctx_ps = psum.tile([P, S], F32, name="ctx_ps_%d" % k, tag="ctx_ps", bufs=2)
+            for a in range(PASSES):
+                nc.tensor.matmul_mx(
+                    out=ctx_ps[:], lhsT=w2_codes[g][:, a, 2 * t * P : 2 * (t + 1) * P].bitcast(FP4X4),
+                    lhsT_scale=w2_sc[g][:, a, t * P : (t + 1) * P],
+                    rhs=v_codes[a][:].bitcast(FP8X4), rhs_scale=v_sc[a][:], start=(a == 0), stop=(a == PASSES - 1),
+                )
+            sym_ps[k] = psum.tile([P, S], F32, name="sym_ps_%d" % k, tag="sym_ps", bufs=3)
+            cols = slice(t * P, (t + 1) * P)
+            for a in range(PASSES):
+                nc.tensor.matmul_mx(
+                    out=sym_ps[k][:], lhsT=w1_codes[g, a][:, cols].bitcast(FP8X4), lhsT_scale=w1_sc[g, a][:, cols],
+                    rhs=v_codes[a][:].bitcast(FP8X4), rhs_scale=v_sc[a][:], start=(a == 0), stop=(a == PASSES - 1),
+                )
+            ctx_sb[k] = sb("ctx_sb_%d" % k, [P, S], F32, tag="ctx_sb", bufs=3)
+            nc.scalar.copy(out=ctx_sb[k][:], in_=ctx_ps[:])
+
+        def meet(k):
+            g, t = divmod(k, PACK)
+            h[k] = sb("h_%d" % k, [P, S], F32, tag="h", bufs=3)
+            nc.vector.scalar_tensor_tensor(
+                out=h[k][:], in0=sym_ps[k][:], scalar=b1_sb[:, g, t : t + 1], in1=ctx_sb[k][:], op0=ALU.add, op1=ALU.max,
+            )
+
+        def scatter(k):
+            nc.vector.tensor_tensor(page[k][:].indirect(idx2[:]), h[k][:], wgs_sb[k % PACK], ALU.mult)
+            nc.sync.dma_start(out=out_rows[k // PACK, k % PACK], in_=page[k][:])
+
+        def pick(k):
+            picked[k] = sb("picked_%d" % k, [P, PICK], F32, tag="picked", bufs=5)
+            nc.vector.tensor_copy(picked[k][:], page[k][:].indirect(idx3[:]))
+
+        page_bf, x_bf = {}, {}
+
+        def round_page(k):
+            g, t = divmod(k, PACK)
+            if t == 0:
+                page_bf[g] = sb("page_bf_%d" % g, [P, PACK, T2], BF16, tag="stage_%d_2" % (1 - g), pool=late)
+            nc.scalar.copy(out=page_bf[g][:, t, :], in_=page[k][:])
+
+        def round_x(k):
+            g, t = divmod(k, PACK)
+            if t == 0:
+                x_bf[g] = sb("x_bf_%d" % g, [P, PACK, PICK], BF16, tag="stage_%d_1" % (1 - g), pool=late)
+            nc.scalar.activation(out=x_bf[g][:, t, :], in_=picked[k][:], func=ACT.Copy, scale=lens_sb[:, g, t : t + 1])
+
+        def weave(engine_copy, dst, src):
+            engine_copy(
+                out=dst.rearrange("p (c i t) -> p c t i", i=4, t=PACK),
+                in_=src.rearrange("p t (c i) -> p c t i", i=4),
+            )
+
+        x_woven, x_codes, x_sc = {}, {}, {}
+
+        def weave_x(g, engine_copy):
+            x_woven[g] = sb("x_woven_%d" % g, [P, PICK * PACK], BF16, tag="x_woven", bufs=1)
+            weave(engine_copy, x_woven[g][:], x_bf[g][:])
+
+        def quantize_x(g):
+            x_codes[g] = sb("x_codes_%d" % g, [P, PICK], U32)
+            x_sc[g] = sb("x_sc_%d" % g, [P, PICK], U8)
+            nc.vector.quantize_mx(out=x_codes[g][:].bitcast(FP8X4), scales=x_sc[g][:], in_=x_woven[g][:])
+
+        page_woven = {}
+        HALF = T2 // 2
+        plane_sc = sb("plane_sc", [P, GROUPS, T2], U8)
+
+        def weave_page(g, half, engine_copy):
+            page_woven[g, half] = sb("page_woven_%d_%d" % (g, half), [P, HALF * PACK], BF16, tag="page_woven", bufs=2)
+            weave(engine_copy, page_woven[g, half][:], page_bf[g][:, :, half * HALF : (half + 1) * HALF])
+
+        def quantize_page(g, half):
+            cols = slice(half * HALF, (half + 1) * HALF)
+            codes = sb("plane_codes_%d_%d" % (g, half), [P, HALF], U32)
+            nc.vector.quantize_mx(out=codes[:].bitcast(FP8X4), scales=plane_sc[:, g, cols], in_=page_woven[g, half][:])
+            nc.sync.dma_start(
+                out=out_2[g].rearrange("p m t -> p (m t)").bitcast(I32)[:, cols], in_=codes[:].bitcast(I32),
+            )
+
+        w3_bf = sb("w3_bf", [P, GROUPS * N * PACK], BF16)
+        w3_codes = sb("w3_codes", [P, GROUPS * N], U32)
+        w3_sc = sb("w3_sc", [P, GROUPS * N], U8)
+
+        def round_w3(g):
+            nc.scalar.copy(
+                out=w3_bf[:, g * N * PACK : (g + 1) * N * PACK].rearrange("p (c m j) -> p m c j", c=N_TILES, j=PACK),
+                in_=w3_raw[g][:].rearrange("p j (m c) -> p m c j", c=N_TILES),
+            )
+
+        def quantize_w3():
+            for lo, hi in ((0, 512), (512, GROUPS * N)):
+                nc.vector.quantize_mx(
+                    out=w3_codes[:, lo:hi].bitcast(FP8X4), scales=w3_sc[:, lo:hi], in_=w3_bf[:, PACK * lo : PACK * hi],
+                )
+
+        e_ps = [psum.tile([P, PICK], F32, name="e_ps_%d" % c) for c in range(N_TILES)]
+
+        def second_stage(g, c):
+            cols = slice(g * N + c * P, g * N + (c + 1) * P)
+            nc.tensor.matmul_mx(
+                out=e_ps[c][:], lhsT=w3_codes[:, cols].bitcast(FP8X4), lhsT_scale=w3_sc[:, cols],
+                rhs=x_codes[g][:].bitcast(FP8X4), rhs_scale=x_sc[g][:], start=(g == 0), stop=(g == GROUPS - 1),
+            )
+
+        first_stage(0)
+        first_stage(1)
+        meet(0)
+        meet(1)
+        scatter(0)
+        first_stage(2)
+        round_w1(1, 0)
+        meet(2)
+        scatter(1)
+        pick(0)
+        quantize_w1(1, 0)
+        first_stage(3)
+        round_w1(1, 1)
+        round_w1(1, 2)
+        meet(3)
+        scatter(2)
+        pick(1)
+        quantize_w1(1, 1)
+        quantize_w1(1, 2)
+        for k in range(2):
+            round_x(k)
+            round_page(k)
+        first_stage(4)
+        scatter(3)
+        pick(2)
+        meet(4)
+        first_stage(5)
+        round_x(2)
+        round_page(2)
+        round_page(3)
+        pick(3)
+        scatter(4)
+        meet(5)
+        first_stage(6)
+        round_x(3)
+        round_w3(0)
+        round_w3(1)
+        weave_x(0, nc.scalar.copy)
+        pick(4)
+        scatter(5)
+        meet(6)
+        first_stage(7)
+        weave_page(0, 0, nc.scalar.copy)
+        round_x(4)
+        round_page(4)
+        quantize_w3()
+        quantize_x(0)
+        for c in range(N_TILES):
+            second_stage(0, c)
+        pick(5)
+        scatter(6)
+        meet(7)
+        weave_page(0, 1, nc.scalar.copy)
+        round_x(5)
+        round_page(5)
+        quantize_page(0, 0)
+        pick(6)
+        round_x(6)
+        round_page(6)
+        x_woven[1] = sb("x_woven_1", [P, PICK * PACK], BF16, tag="x_woven", bufs=1)
+        nc.scalar.copy(
+            out=x_woven[1][:].rearrange("p (c i t) -> p c t i", i=4, t=PACK)[:, :, 0:3, :],
+            in_=x_bf[1][:, 0:3, :].rearrange("p t (c i) -> p c t i", i=4),
+        )
+        quantize_page(0, 1)
+        scatter(7)
+        pick(7)
+        round_page(7)
+        nc.scalar.activation(
+            out=x_woven[1][:].rearrange("p (c t) -> p c t", t=PACK)[:, :, 3], in_=picked[7][:], func=ACT.Copy,
+            scale=lens_sb[:, 1, 3:4],
+        )
+        weave_page(1, 0, nc.vector.tensor_copy)
+        quantize_x(1)
+        page_woven[1, 1] = sb("page_woven_1_1", [P, HALF * PACK], BF16, tag="page_woven", bufs=2)
+        QUART = HALF // 2
+        weave(nc.scalar.copy, page_woven[1, 1][:, QUART * PACK :], page_bf[1][:, :, HALF + QUART :])
+        out_0_rows = out_0.rearrange("(p c) j -> c p j", c=N_TILES)
+        for c in range(N_TILES):
+            second_stage(1, c)
+            y = sb("y_%d" % c, [P, PICK], F32, tag="ctx_sb", bufs=3)
+            nc.scalar.activation(out=y[:], in_=e_ps[c][:], func=ACT.Sigmoid, bias=b3_sb[:, c : c + 1])
+            nc.sync.dma_start(out=out_0_rows[c], in_=y[:])
+        quantize_page(1, 0)
+        weave(nc.vector.tensor_copy, page_woven[1, 1][:, : QUART * PACK], page_bf[1][:, :, HALF : HALF + QUART])
+        quantize_page(1, 1)
+        for q in range(QUADS):
+            nc.sync.dma_start(
+                out=out_3[:, 4 * q : 4 * q + 4, :].bitcast(I32).rearrange("g r m -> r g m"),
+                in_=plane_sc[QUAD * q : QUAD * q + 4, :, :].bitcast(I32),
+            )

@@ -1,6 +1,7 @@
 from contextlib import ExitStack
 
 import concourse.mybir as mybir
+from concourse.masks import make_identity
 
 K, H, N, T, S, T2, PICK = 1536, 1024, 384, 2048, 512, 1024, 512
 FLOPS = 2 * (2 * K * H * S + H * N * PICK)
@@ -76,17 +77,12 @@ def tile_list_triage_urgency_marks_kernel(
             page[k] = sb("page_%d" % k, [P, T2], F32, pool=late)
             nc.sync.dma_start(out=page[k][:], in_=page_rows[k // PACK, k % PACK])
 
-        wgs_rows = wgs.rearrange("(q t) j -> q t j", t=PACK)
-        wgs_sb = {}
+        w2_raw, w2_codes, w2_sc = {}, {}, {}
 
-        def load_wgs(t0, t1):
-            part = sb("wgs_%d" % t0, [P, t1 - t0, S], F32, pool=late)
-            for q in (0, 2, 1, 3):
-                nc.sync.dma_start(out=part[QUAD * q : QUAD * (q + 1), :, :], in_=wgs_rows[:, t0:t1, :])
-            for t in range(t0, t1):
-                wgs_sb[t] = part[:, t - t0, :]
-
-        w2_codes, w2_sc = {}, {}
+        def load_w2(g, pool):
+            w2_raw[g] = sb("w2_raw_%d" % g, [P, PASSES, K_PASS // 2], I32, pool=pool)
+            words = w2_words[:, :, g * 2 * K_PASS : (g + 1) * 2 * K_PASS]
+            nc.sync.dma_start(out=w2_raw[g][:], in_=words.bitcast(I32).rearrange("a p c -> p a c"))
 
         def deal_w2_words(g):
             w2_codes[g] = sb("w2_codes_%d" % g, [P, PASSES, K_PASS * 2], U8)
@@ -96,12 +92,10 @@ def tile_list_triage_urgency_marks_kernel(
             )
 
         with tc.tile_pool(name="early", bufs=1) as early:
-            w2_raw = {}
-            for g in range(GROUPS):
-                w2_raw[g] = sb("w2_raw_%d" % g, [P, PASSES, K_PASS // 2], I32, pool=early if g == 0 else keep)
-                words = w2_words[:, :, g * 2 * K_PASS : (g + 1) * 2 * K_PASS]
-                nc.sync.dma_start(out=w2_raw[g][:], in_=words.bitcast(I32).rearrange("a p c -> p a c"))
+            load_w2(0, early)
             nc.sync.dma_start(idx[:], offs)
+            wgs_raw = sb("wgs_raw", [P, S], F32)
+            nc.sync.dma_start(out=wgs_raw[:], in_=wgs)
             nc.sync.dma_start(idx2[:], offs2)
             nc.sync.dma_start(idx3[:], offs3)
             for q in range(QUADS):
@@ -115,36 +109,50 @@ def tile_list_triage_urgency_marks_kernel(
                     in_=w2_scales[:, 4 * q : 4 * q + 4, :].bitcast(I32).rearrange("a r c -> r a c"),
                 )
             deal_w2_words(0)
-        deal_w2_words(1)
         late = ctx.enter_context(tc.tile_pool(name="late", bufs=1))
+        ident = sb("ident", [P, P], F32)
+        make_identity(nc, ident[:])
+        CHUNKS = S // P
+        wgs_t = psum.tile([P, CHUNKS, P], F32, name="wgs_t", tag="e_ps_0")
+        for c in range(CHUNKS):
+            nc.tensor.transpose(wgs_t[:, c, :], wgs_raw[:, c * P : (c + 1) * P], ident[:])
+        wgs_spread = sb("wgs_spread", [P, CHUNKS, PACK, QUADS, QUAD], F32, tag="stage_1_2", pool=late)
+        for u in range(QUADS):
+            nc.scalar.copy(out=wgs_spread[:, :, :, u, :], in_=wgs_t[:].rearrange("p c (q t) -> p c t q", t=PACK))
+        wgs_sb = {}
+        for t in range(PACK):
+            back = psum.tile([P, CHUNKS, P], F32, name="wgs_back_%d" % t, tag="e_ps_%d" % ((t + 1) % N_TILES))
+            for c in range(CHUNKS):
+                nc.tensor.transpose(back[:, c, :], wgs_spread[:, c, t].rearrange("p u q -> p (u q)"), ident[:])
+            dealt = sb("wgs_%d" % t, [P, S], F32)
+            nc.scalar.copy(out=dealt[:], in_=back[:].rearrange("p c j -> p (c j)"))
+            wgs_sb[t] = dealt[:]
+
         load_w1(0, 0, late)
         load_w1(0, 1, late)
         load_tab(0)
         load_w1(0, 2, late)
         load_tab(1)
         load_tab(2)
+        load_w2(1, late)
         b1_sb = sb("b1_sb", [P, GROUPS, PACK], F32, pool=late)
         nc.sync.dma_start(out=b1_sb[:], in_=b1.rearrange("(g p t) -> p g t", p=P, t=PACK))
         load_page(0)
-        load_wgs(0, 1)
+        load_w1(1, 0, late)
         load_page(1)
+        load_w1(1, 1, late)
+        load_w1(1, 2, late)
+        load_page(2)
         lens_sb = sb("lens_sb", [P, GROUPS, PACK], F32, pool=late)
         nc.sync.dma_start(out=lens_sb[:], in_=lens.rearrange("(g p t) -> p g t", p=P, t=PACK))
         b3_sb = sb("b3_sb", [P, N_TILES], F32, pool=late)
         nc.sync.dma_start(out=b3_sb[:], in_=b3.rearrange("(p c) -> p c", c=N_TILES))
-        load_wgs(1, 2)
-        load_w1(1, 0, late)
-        load_wgs(2, 4)
-        load_page(2)
-        load_w1(1, 1, late)
-        load_w1(1, 2, late)
-        load_page(3)
-        load_page(4)
         w3_raw = {}
         for g in range(GROUPS):
             rows = w3[g * K_PASS : (g + 1) * K_PASS, :]
-            w3_raw[g] = sb("w3_raw_%d" % g, [P, PACK, N], F32, pool=late)
+            w3_raw[g] = sb("w3_raw_%d" % g, [P, PACK, N], F32, tag=None if g else "tab_0", pool=late)
             nc.sync.dma_start(out=w3_raw[g][:], in_=rows.rearrange("(p j) n -> p j n", j=PACK))
+            load_page(3 + g)
         for k in range(5, TILES):
             load_page(k)
 
@@ -187,6 +195,7 @@ def tile_list_triage_urgency_marks_kernel(
             quantize_w1(0, a)
             gather_words(a)
         deal_w2_scales(1)
+        deal_w2_words(1)
 
         h, picked, sym_ps, ctx_sb = {}, {}, {}, {}
 
@@ -229,13 +238,13 @@ def tile_list_triage_urgency_marks_kernel(
         def round_page(k):
             g, t = divmod(k, PACK)
             if t == 0:
-                page_bf[g] = sb("page_bf_%d" % g, [P, PACK, T2], BF16, tag="stage_%d_2" % (1 - g), pool=late)
+                page_bf[g] = sb("page_bf_%d" % g, [P, PACK, T2], BF16, tag="stage_0_2" if g else "w3_raw_1", pool=late)
             nc.scalar.copy(out=page_bf[g][:, t, :], in_=page[k][:])
 
         def round_x(k):
             g, t = divmod(k, PACK)
             if t == 0:
-                x_bf[g] = sb("x_bf_%d" % g, [P, PACK, PICK], BF16, tag="stage_%d_1" % (1 - g), pool=late)
+                x_bf[g] = sb("x_bf_%d" % g, [P, PACK, PICK], BF16, tag="stage_0_1" if g else "stage_1_2", pool=late)
             nc.scalar.activation(out=x_bf[g][:, t, :], in_=picked[k][:], func=ACT.Copy, scale=lens_sb[:, g, t : t + 1])
 
         def weave(engine_copy, dst, src):
@@ -271,7 +280,7 @@ def tile_list_triage_urgency_marks_kernel(
                 out=out_2[g].rearrange("p m t -> p (m t)").bitcast(I32)[:, cols], in_=codes[:].bitcast(I32),
             )
 
-        w3_bf = sb("w3_bf", [P, GROUPS * N * PACK], BF16)
+        w3_bf = sb("w3_bf", [P, GROUPS * N * PACK], BF16, tag="tab_1", pool=late)
         w3_codes = sb("w3_codes", [P, GROUPS * N], U32)
         w3_sc = sb("w3_sc", [P, GROUPS * N], U8)
 
@@ -287,7 +296,7 @@ def tile_list_triage_urgency_marks_kernel(
                     out=w3_codes[:, lo:hi].bitcast(FP8X4), scales=w3_sc[:, lo:hi], in_=w3_bf[:, PACK * lo : PACK * hi],
                 )
 
-        e_ps = [psum.tile([P, PICK], F32, name="e_ps_%d" % c) for c in range(N_TILES)]
+        e_ps = [psum.tile([P, PICK], F32, name="e_ps_%d" % c, tag="e_ps_%d" % c) for c in range(N_TILES)]
 
         def second_stage(g, c):
             cols = slice(g * N + c * P, g * N + (c + 1) * P)
@@ -315,10 +324,12 @@ def tile_list_triage_urgency_marks_kernel(
         pick(1)
         quantize_w1(1, 1)
         quantize_w1(1, 2)
+        first_stage(4)
+        round_w3(0)
+        round_w3(1)
         for k in range(2):
             round_x(k)
             round_page(k)
-        first_stage(4)
         scatter(3)
         pick(2)
         meet(4)
@@ -331,8 +342,6 @@ def tile_list_triage_urgency_marks_kernel(
         meet(5)
         first_stage(6)
         round_x(3)
-        round_w3(0)
-        round_w3(1)
         weave_x(0, nc.scalar.copy)
         pick(4)
         scatter(5)

from contextlib import ExitStack

import concourse.mybir as mybir
from concourse.masks import make_identity

K, H, N, T, S, T2, PICK = 1536, 1024, 384, 2048, 512, 1024, 512
FLOPS = 2 * (2 * K * H * S + H * N * PICK)

F32 = mybir.dt.float32
BF16 = mybir.dt.bfloat16
I32 = mybir.dt.int32
U32 = mybir.dt.uint32
U16 = mybir.dt.uint16
U8 = mybir.dt.uint8
FP8X4 = mybir.dt.float8_e4m3fn_x4
FP4X4 = mybir.dt.float4_e2m1fn_x4
ALU = mybir.AluOpType
ACT = mybir.ActivationFunctionType

P = 128
PACK = 4
K_PASS = P * PACK
PASSES = K // K_PASS
GROUPS = H // K_PASS
TILES = GROUPS * PACK
N_TILES = N // P
QUADS = 4
QUAD = 32


def tile_list_triage_urgency_marks_kernel(
    tc, tab_words, tab_scales, offs, offs2, offs3, w1, b1, w2_words, w2_scales, wgs, page0, lens, w3, b3,
    out_0, out_1, out_2, out_3,
):
    nc = tc.nc
    with ExitStack() as ctx:
        lists = ctx.enter_context(tc.tile_pool(name="lists", bufs=1))
        keep = ctx.enter_context(tc.tile_pool(name="keep", bufs=1))
        psum = ctx.enter_context(tc.psum_pool(name="psum", bufs=1))

        def sb(name, shape, dtype, tag=None, bufs=1, pool=keep):
            return pool.tile(shape, dtype, name=name, tag=tag or name, bufs=bufs, align_bytes=64)

        idx = lists.tile([P, S // 16], U16, name="idx")
        idx2 = lists.tile([P, S // 16], U16, name="idx2")
        idx3 = lists.tile([P, PICK // 16], U16, name="idx3")

        tab_sc = sb("tab_sc", [P, PASSES, T], U8)
        w2_sc_raw = sb("w2_sc_raw", [P, PASSES, H], U8)
        nc.vector.memset(tab_sc[:].bitcast(I32), 0)
        nc.vector.memset(w2_sc_raw[:].bitcast(I32), 0)

        warm = sb("warm", [P, 8], F32)
        nc.vector.memset(warm[:], 0.0)
        nc.scalar.activation(out=warm[:, 1:2], in_=warm[:, 0:1], func=ACT.Sigmoid)

        w1_raw = {}

        def load_w1(g, a, pool):
            raw = sb("w1_raw_%d_%d" % (g, a), [P, PACK, K_PASS], F32, tag="stage_%d_%d" % (g, a), pool=pool)
            rows = w1[a * K_PASS : (a + 1) * K_PASS, g * K_PASS : (g + 1) * K_PASS]
            nc.sync.dma_start(out=raw[:], in_=rows.rearrange("(p j) c -> p j c", j=PACK))
            w1_raw[g, a] = raw

        tab = {}

        def load_tab(a):
            words = sb("tab_%d" % a, [P, T], I32, pool=late)
            nc.sync.dma_start(out=words[:], in_=tab_words[a].rearrange("p t i -> p (t i)").bitcast(I32))
            tab[a] = words

        page = {}
        page_rows = page0.rearrange("(g p t) m -> g t p m", p=P, t=PACK)
        out_rows = out_1.rearrange("(g p t) m -> g t p m", p=P, t=PACK)

        def load_page(k):
            page[k] = sb("page_%d" % k, [P, T2], F32, pool=late)
            nc.sync.dma_start(out=page[k][:], in_=page_rows[k // PACK, k % PACK])

        w2_raw, w2_codes, w2_sc = {}, {}, {}

        def load_w2(g, pool):
            w2_raw[g] = sb("w2_raw_%d" % g, [P, PASSES, K_PASS // 2], I32, pool=pool)
            words = w2_words[:, :, g * 2 * K_PASS : (g + 1) * 2 * K_PASS]
            nc.sync.dma_start(out=w2_raw[g][:], in_=words.bitcast(I32).rearrange("a p c -> p a c"))

        def deal_w2_words(g):
            w2_codes[g] = sb("w2_codes_%d" % g, [P, PASSES, K_PASS * 2], U8)
            nc.vector.tensor_copy(
                out=w2_codes[g][:].bitcast(U16).rearrange("p a (t h i) -> p h a t i", t=PACK, i=8),
                in_=w2_raw[g][:].bitcast(U16).rearrange("p a (h i t) -> p h a t i", t=PACK, i=8),
            )

        with tc.tile_pool(name="early", bufs=1) as early:
            load_w2(0, early)
            nc.sync.dma_start(idx[:], offs)
            wgs_raw = sb("wgs_raw", [P, S], F32)
            nc.sync.dma_start(out=wgs_raw[:], in_=wgs)
            nc.sync.dma_start(idx2[:], offs2)
            nc.sync.dma_start(idx3[:], offs3)
            for q in range(QUADS):
                nc.sync.dma_start(
                    out=tab_sc[QUAD * q : QUAD * q + 4, :, :].bitcast(I32),
                    in_=tab_scales[:, 4 * q : 4 * q + 4, :].bitcast(I32).rearrange("a r t -> r a t"),
                )
            for q in range(QUADS):
                nc.sync.dma_start(
                    out=w2_sc_raw[QUAD * q : QUAD * q + 4, :, :].bitcast(I32),
                    in_=w2_scales[:, 4 * q : 4 * q + 4, :].bitcast(I32).rearrange("a r c -> r a c"),
                )
            deal_w2_words(0)
        late = ctx.enter_context(tc.tile_pool(name="late", bufs=1))
        ident = sb("ident", [P, P], F32)
        make_identity(nc, ident[:])
        CHUNKS = S // P
        wgs_t = psum.tile([P, CHUNKS, P], F32, name="wgs_t", tag="e_ps_0")
        for c in range(CHUNKS):
            nc.tensor.transpose(wgs_t[:, c, :], wgs_raw[:, c * P : (c + 1) * P], ident[:])
        wgs_spread = sb("wgs_spread", [P, CHUNKS, PACK, QUADS, QUAD], F32, tag="stage_1_2", pool=late)
        for u in range(QUADS):
            nc.scalar.copy(out=wgs_spread[:, :, :, u, :], in_=wgs_t[:].rearrange("p c (q t) -> p c t q", t=PACK))
        wgs_sb = {}
        for t in range(PACK):
            back = psum.tile([P, CHUNKS, P], F32, name="wgs_back_%d" % t, tag="e_ps_%d" % ((t + 1) % N_TILES))
            for c in range(CHUNKS):
                nc.tensor.transpose(back[:, c, :], wgs_spread[:, c, t].rearrange("p u q -> p (u q)"), ident[:])
            dealt = sb("wgs_%d" % t, [P, S], F32)
            nc.scalar.copy(out=dealt[:], in_=back[:].rearrange("p c j -> p (c j)"))
            wgs_sb[t] = dealt[:]

        load_w1(0, 0, late)
        load_w1(0, 1, late)
        load_tab(0)
        load_w1(0, 2, late)
        load_tab(1)
        load_tab(2)
        load_w2(1, late)
        b1_sb = sb("b1_sb", [P, GROUPS, PACK], F32, pool=late)
        nc.sync.dma_start(out=b1_sb[:], in_=b1.rearrange("(g p t) -> p g t", p=P, t=PACK))
        load_page(0)
        load_w1(1, 0, late)
        load_page(1)
        load_w1(1, 1, late)
        load_w1(1, 2, late)
        load_page(2)
        lens_sb = sb("lens_sb", [P, GROUPS, PACK], F32, pool=late)
        nc.sync.dma_start(out=lens_sb[:], in_=lens.rearrange("(g p t) -> p g t", p=P, t=PACK))
        b3_sb = sb("b3_sb", [P, N_TILES], F32, pool=late)
        nc.sync.dma_start(out=b3_sb[:], in_=b3.rearrange("(p c) -> p c", c=N_TILES))
        w3_raw = {}
        for g in range(GROUPS):
            rows = w3[g * K_PASS : (g + 1) * K_PASS, :]
            w3_raw[g] = sb("w3_raw_%d" % g, [P, PACK, N], F32, tag=None if g else "tab_0", pool=late)
            nc.sync.dma_start(out=w3_raw[g][:], in_=rows.rearrange("(p j) n -> p j n", j=PACK))
            load_page(3 + g)
        for k in range(5, TILES):
            load_page(k)

        w1_codes, w1_sc, w1_bf = {}, {}, {}

        def round_w1(g, a):
            w1_bf[g, a] = sb("w1_bf_%d_%d" % (g, a), [P, K_PASS * PACK], BF16, tag="w1_bf", bufs=2)
            nc.scalar.copy(
                out=w1_bf[g, a][:].rearrange("p (t m j) -> p m t j", t=PACK, j=PACK),
                in_=w1_raw[g, a][:].rearrange("p j (m t) -> p m t j", t=PACK),
            )

        def quantize_w1(g, a):
            w1_codes[g, a] = sb("w1_codes_%d_%d" % (g, a), [P, K_PASS], U32)
            w1_sc[g, a] = sb("w1_sc_%d_%d" % (g, a), [P, K_PASS], U8)
            nc.vector.quantize_mx(out=w1_codes[g, a][:].bitcast(FP8X4), scales=w1_sc[g, a][:], in_=w1_bf[g, a][:])

        v_codes, v_sc = {}, {}

        def gather_scales(a):
            v_sc[a] = sb("v_sc_%d" % a, [P, S], U8)
            nc.vector.tensor_copy(v_sc[a][:], tab_sc[:, a, :].indirect(idx[:]))

        def gather_words(a):
            v_codes[a] = sb("v_codes_%d" % a, [P, S], U32)
            nc.vector.tensor_copy(v_codes[a][:], tab[a][:].bitcast(U32).indirect(idx[:]))

        def deal_w2_scales(g):
            w2_sc[g] = sb("w2_sc_%d" % g, [P, PASSES, K_PASS], U8, tag="tab_2" if g else None, pool=late)
            nc.vector.tensor_copy(
                out=w2_sc[g][:].rearrange("p a (t h i) -> p h a t i", t=PACK, i=16),
                in_=w2_sc_raw[:, :, g * K_PASS : (g + 1) * K_PASS].rearrange("p a (h i t) -> p h a t i", t=PACK, i=16),
            )

        for a in range(PASSES):
            gather_scales(a)
        deal_w2_scales(0)
        for a in range(PASSES):
            round_w1(0, a)
            quantize_w1(0, a)
            gather_words(a)
        deal_w2_scales(1)
        deal_w2_words(1)

        h, picked, sym_ps, ctx_sb = {}, {}, {}, {}

        def first_stage(k):
            g, t = divmod(k, PACK)
            ctx_ps = psum.tile([P, S], F32, name="ctx_ps_%d" % k, tag="ctx_ps", bufs=2)
            for a in range(PASSES):
                nc.tensor.matmul_mx(
                    out=ctx_ps[:], lhsT=w2_codes[g][:, a, 2 * t * P : 2 * (t + 1) * P].bitcast(FP4X4),
                    lhsT_scale=w2_sc[g][:, a, t * P : (t + 1) * P],
                    rhs=v_codes[a][:].bitcast(FP8X4), rhs_scale=v_sc[a][:], start=(a == 0), stop=(a == PASSES - 1),
                )
            sym_ps[k] = psum.tile([P, S], F32, name="sym_ps_%d" % k, tag="sym_ps", bufs=3)
            cols = slice(t * P, (t + 1) * P)
            for a in range(PASSES):
                nc.tensor.matmul_mx(
                    out=sym_ps[k][:], lhsT=w1_codes[g, a][:, cols].bitcast(FP8X4), lhsT_scale=w1_sc[g, a][:, cols],
                    rhs=v_codes[a][:].bitcast(FP8X4), rhs_scale=v_sc[a][:], start=(a == 0), stop=(a == PASSES - 1),
                )
            ctx_sb[k] = sb("ctx_sb_%d" % k, [P, S], F32, tag="ctx_sb", bufs=3)
            nc.scalar.copy(out=ctx_sb[k][:], in_=ctx_ps[:])

        def meet(k):
            g, t = divmod(k, PACK)
            h[k] = sb("h_%d" % k, [P, S], F32, tag="h", bufs=3)
            nc.vector.scalar_tensor_tensor(
                out=h[k][:], in0=sym_ps[k][:], scalar=b1_sb[:, g, t : t + 1], in1=ctx_sb[k][:], op0=ALU.add, op1=ALU.max,
            )

        def scatter(k):
            nc.vector.tensor_tensor(page[k][:].indirect(idx2[:]), h[k][:], wgs_sb[k % PACK], ALU.mult)
            nc.sync.dma_start(out=out_rows[k // PACK, k % PACK], in_=page[k][:])

        def pick(k):
            picked[k] = sb("picked_%d" % k, [P, PICK], F32, tag="picked", bufs=5)
            nc.vector.tensor_copy(picked[k][:], page[k][:].indirect(idx3[:]))

        page_bf, x_bf = {}, {}

        def round_page(k):
            g, t = divmod(k, PACK)
            if t == 0:
                page_bf[g] = sb("page_bf_%d" % g, [P, PACK, T2], BF16, tag="stage_0_2" if g else "w3_raw_1", pool=late)
            nc.scalar.copy(out=page_bf[g][:, t, :], in_=page[k][:])

        def round_x(k):
            g, t = divmod(k, PACK)
            if t == 0:
                x_bf[g] = sb("x_bf_%d" % g, [P, PACK, PICK], BF16, tag="stage_0_1" if g else "stage_1_2", pool=late)
            nc.scalar.activation(out=x_bf[g][:, t, :], in_=picked[k][:], func=ACT.Copy, scale=lens_sb[:, g, t : t + 1])

        def weave(engine_copy, dst, src):
            engine_copy(
                out=dst.rearrange("p (c i t) -> p c t i", i=4, t=PACK),
                in_=src.rearrange("p t (c i) -> p c t i", i=4),
            )

        x_woven, x_codes, x_sc = {}, {}, {}

        def weave_x(g, engine_copy):
            x_woven[g] = sb("x_woven_%d" % g, [P, PICK * PACK], BF16, tag="x_woven", bufs=1)
            weave(engine_copy, x_woven[g][:], x_bf[g][:])

        def quantize_x(g):
            x_codes[g] = sb("x_codes_%d" % g, [P, PICK], U32)
            x_sc[g] = sb("x_sc_%d" % g, [P, PICK], U8)
            nc.vector.quantize_mx(out=x_codes[g][:].bitcast(FP8X4), scales=x_sc[g][:], in_=x_woven[g][:])

        page_woven = {}
        HALF = T2 // 2
        plane_sc = sb("plane_sc", [P, GROUPS, T2], U8)

        def weave_page(g, half, engine_copy):
            page_woven[g, half] = sb("page_woven_%d_%d" % (g, half), [P, HALF * PACK], BF16, tag="page_woven", bufs=2)
            weave(engine_copy, page_woven[g, half][:], page_bf[g][:, :, half * HALF : (half + 1) * HALF])

        def quantize_page(g, half):
            cols = slice(half * HALF, (half + 1) * HALF)
            codes = sb("plane_codes_%d_%d" % (g, half), [P, HALF], U32)
            nc.vector.quantize_mx(out=codes[:].bitcast(FP8X4), scales=plane_sc[:, g, cols], in_=page_woven[g, half][:])
            nc.sync.dma_start(
                out=out_2[g].rearrange("p m t -> p (m t)").bitcast(I32)[:, cols], in_=codes[:].bitcast(I32),
            )

        w3_bf = sb("w3_bf", [P, GROUPS * N * PACK], BF16, tag="tab_1", pool=late)
        w3_codes = sb("w3_codes", [P, GROUPS * N], U32)
        w3_sc = sb("w3_sc", [P, GROUPS * N], U8)

        def round_w3(g):
            nc.scalar.copy(
                out=w3_bf[:, g * N * PACK : (g + 1) * N * PACK].rearrange("p (c m j) -> p m c j", c=N_TILES, j=PACK),
                in_=w3_raw[g][:].rearrange("p j (m c) -> p m c j", c=N_TILES),
            )

        def quantize_w3():
            for lo, hi in ((0, 512), (512, GROUPS * N)):
                nc.vector.quantize_mx(
                    out=w3_codes[:, lo:hi].bitcast(FP8X4), scales=w3_sc[:, lo:hi], in_=w3_bf[:, PACK * lo : PACK * hi],
                )

        e_ps = [psum.tile([P, PICK], F32, name="e_ps_%d" % c, tag="e_ps_%d" % c) for c in range(N_TILES)]

        def second_stage(g, c):
            cols = slice(g * N + c * P, g * N + (c + 1) * P)
            nc.tensor.matmul_mx(
                out=e_ps[c][:], lhsT=w3_codes[:, cols].bitcast(FP8X4), lhsT_scale=w3_sc[:, cols],
                rhs=x_codes[g][:].bitcast(FP8X4), rhs_scale=x_sc[g][:], start=(g == 0), stop=(g == GROUPS - 1),
            )

        first_stage(0)
        first_stage(1)
        meet(0)
        meet(1)
        scatter(0)
        first_stage(2)
        round_w1(1, 0)
        meet(2)
        scatter(1)
        pick(0)
        quantize_w1(1, 0)
        first_stage(3)
        round_w1(1, 1)
        round_w1(1, 2)
        meet(3)
        scatter(2)
        pick(1)
        quantize_w1(1, 1)
        quantize_w1(1, 2)
        first_stage(4)
        round_w3(0)
        round_w3(1)
        for k in range(2):
            round_x(k)
            round_page(k)
        scatter(3)
        pick(2)
        meet(4)
        first_stage(5)
        round_x(2)
        round_page(2)
        round_page(3)
        pick(3)
        scatter(4)
        meet(5)
        first_stage(6)
        round_x(3)
        weave_x(0, nc.scalar.copy)
        pick(4)
        scatter(5)
        meet(6)
        first_stage(7)
        weave_page(0, 0, nc.scalar.copy)
        round_x(4)
        round_page(4)
        quantize_w3()
        quantize_x(0)
        for c in range(N_TILES):
            second_stage(0, c)
        pick(5)
        scatter(6)
        meet(7)
        weave_page(0, 1, nc.scalar.copy)
        round_x(5)
        round_page(5)
        quantize_page(0, 0)
        pick(6)
        round_x(6)
        round_page(6)
        x_woven[1] = sb("x_woven_1", [P, PICK * PACK], BF16, tag="x_woven", bufs=1)
        nc.scalar.copy(
            out=x_woven[1][:].rearrange("p (c i t) -> p c t i", i=4, t=PACK)[:, :, 0:3, :],
            in_=x_bf[1][:, 0:3, :].rearrange("p t (c i) -> p c t i", i=4),
        )
        quantize_page(0, 1)
        scatter(7)
        pick(7)
        round_page(7)
        nc.scalar.activation(
            out=x_woven[1][:].rearrange("p (c t) -> p c t", t=PACK)[:, :, 3], in_=picked[7][:], func=ACT.Copy,
            scale=lens_sb[:, 1, 3:4],
        )
        weave_page(1, 0, nc.vector.tensor_copy)
        quantize_x(1)
        page_woven[1, 1] = sb("page_woven_1_1", [P, HALF * PACK], BF16, tag="page_woven", bufs=2)
        QUART = HALF // 2
        weave(nc.scalar.copy, page_woven[1, 1][:, QUART * PACK :], page_bf[1][:, :, HALF + QUART :])
        out_0_rows = out_0.rearrange("(p c) j -> c p j", c=N_TILES)
        for c in range(N_TILES):
            second_stage(1, c)
            y = sb("y_%d" % c, [P, PICK], F32, tag="ctx_sb", bufs=3)
            nc.scalar.activation(out=y[:], in_=e_ps[c][:], func=ACT.Sigmoid, bias=b3_sb[:, c : c + 1])
            nc.sync.dma_start(out=out_0_rows[c], in_=y[:])
        quantize_page(1, 0)
        weave(nc.vector.tensor_copy, page_woven[1, 1][:, : QUART * PACK], page_bf[1][:, :, HALF : HALF + QUART])
        quantize_page(1, 1)
        for q in range(QUADS):
            nc.sync.dma_start(
                out=out_3[:, 4 * q : 4 * q + 4, :].bitcast(I32).rearrange("g r m -> r g m"),
                in_=plane_sc[QUAD * q : QUAD * q + 4, :, :].bitcast(I32),
            )
